import numpy as np
import ml_dtypes


def mxq(x, axis, fmt="e4m3"):
    dtype, down = {"e4m3": (ml_dtypes.float8_e4m3fn, 7), "e5m2": (ml_dtypes.float8_e5m2, 14)}[fmt]
    v = np.moveaxis(np.asarray(x, np.float32).astype(ml_dtypes.bfloat16).astype(np.float64), axis, -1)
    blocks = v.reshape(v.shape[:-1] + (-1, 32))
    amax = np.abs(blocks).max(-1, keepdims=True)
    byte = np.maximum(np.where(amax > 0, np.frexp(amax)[1] - 1 + 127, 0) - down, 1)
    scale = np.exp2(byte - 127.0)
    codes = (blocks / scale).astype(np.float32).astype(dtype).astype(np.float64)
    return np.moveaxis((codes * scale).reshape(v.shape), -1, axis)


WIDE = False


def mx_kscale(k):
    if not WIDE:
        return np.ones(k)
    levels = np.array([10, -10, 5, -5, 0])
    if k % 512:
        return np.exp2(np.random.permutation(np.resize(levels, k // 32))).repeat(32)
    a = np.empty((k // 512, 16))
    for p in range(k // 512):
        a[p, :8] = np.random.permutation(np.resize(levels, 8))
        for g in range(8):
            far = levels[np.abs(levels - a[p, g]) >= 10]
            a[p, g + 8] = far[np.random.randint(len(far))]
    return np.exp2(a.ravel()).repeat(32)


def f64(x):
    return np.asarray(x).astype(np.float64)


def striped(idx):
    return np.tile(idx.reshape(-1, 16).T, (8, 1)).astype(np.uint16)


def unstriped(offs):
    return offs[:16].T.reshape(-1).astype(np.int64)


def striped8(idx):
    return np.concatenate([x.reshape(-1, 16).T for x in idx]).astype(np.uint16)


def runs(offs, k):
    lists = np.stack([offs[16 * r : 16 * r + 16].T.reshape(-1) for r in range(8)]).astype(np.int64)
    return lists[np.arange(k) % 512 // 64]


def pack_weight(w):
    k, n = w.shape
    w = f64(np.asarray(w, np.float32).astype(ml_dtypes.bfloat16)).reshape(k // 32, 32, n)
    amax = np.abs(w).max(1)
    byte = np.clip(np.where(amax > 0, np.frexp(amax)[1] - 1 + 127 - 7, 1), 1, 254)
    scaled = (w * np.exp2(127.0 - byte)[:, None, :]).reshape(k, n).astype(np.float32)
    words = np.ascontiguousarray(scaled.reshape(k // 512, 128, 4, n).transpose(0, 1, 3, 2)).astype(ml_dtypes.float8_e4m3fn).view(np.uint8)
    return words, np.ascontiguousarray(byte.astype(np.uint8).reshape(k // 512, 16, n))


def unpack_weight(words, scales):
    g, p, n, _ = words.shape
    vals = np.ascontiguousarray(words).view(ml_dtypes.float8_e4m3fn).astype(np.float64) * np.repeat(np.exp2(scales.astype(np.float64) - 127.0), 8, axis=1)[..., None]
    return vals.transpose(0, 1, 3, 2).reshape(g * 512, n)

def planes(y):
    n, m = y.shape
    v = y.astype(np.float32).astype(ml_dtypes.bfloat16).astype(np.float64).reshape(n // 32, 32, m)
    top = np.abs(v).max(1)
    byte = np.clip(np.where(top > 0, np.frexp(top)[1] - 1 + 127 - 7, 1), 1, 254)
    codes = (v * np.exp2(127.0 - byte)[:, None, :]).reshape(n, m).astype(np.float32).astype(ml_dtypes.float8_e4m3fn).view(np.uint8)
    words = codes.reshape(n // 512, 128, 4, m).transpose(0, 1, 3, 2)
    return np.ascontiguousarray(words), np.ascontiguousarray(byte.astype(np.uint8).reshape(n // 512, 16, m))


K, T, S, N, G, H, J = 512, 1024, 256, 512, 2048, 512, 512


def setup_inputs():
    n = np.random.standard_normal
    s = mx_kscale(K)[:, None]
    u = mx_kscale(K)
    packed_xT = pack_weight(n((K, T)) * s)
    packed_dT = pack_weight(n((K, G)) / s)
    packed_w1 = pack_weight(n((H, N)) / np.sqrt(2 * H) / u[:, None])
    packed_w2 = pack_weight(n((H, N)) / np.sqrt(2 * H) / u[:, None])
    return {
        "x_words": packed_xT[0],
        "x_scales": packed_xT[1],
        "d_words": packed_dT[0],
        "d_scales": packed_dT[1],
        "tab": n((H, J)).astype(np.float32),
        "gn": (np.random.uniform(0.5, 1.5, (H, 1)) * u[:, None]).astype(np.float32),
        "gm": (np.random.uniform(0.5, 1.5, (H, 1)) * u[:, None]).astype(np.float32),
        "w1_words": packed_w1[0],
        "w1_scales": packed_w1[1],
        "w2_words": packed_w2[0],
        "w2_scales": packed_w2[1],
        "offs": striped(np.random.permutation(T)[:S]),
        "k1": striped8(np.random.randint(0, G, (8, H))),
        "two": striped(np.random.permutation(T)[:S]),
        "k2": striped8(np.random.randint(0, G, (8, H))),
        "n1": striped(np.random.permutation(S)),
        "n2": striped(np.random.permutation(S)),
        "n3": striped(np.random.randint(0, J, S)),
        "n4": striped(np.random.permutation(S)),
        "n5": striped(np.random.permutation(S)),
        "n6": striped(np.random.permutation(S)),
        "n7": striped(np.random.permutation(S)),
    }


def reference(x_words, x_scales, d_words, d_scales, tab, gn, gm, w1_words, w1_scales, w2_words, w2_scales, offs, k1, two, k2, n1, n2, n3, n4, n5, n6, n7):
    d_k1 = unpack_weight(d_words, d_scales)[np.arange(K)[:, None], runs(k1, K)]
    xq = unpack_weight(x_words, x_scales)[:, unstriped(offs)]
    a = 0.0625 * (d_k1.T @ xq)
    z = f64(gn) * ((a - a[:, unstriped(n1)]) / (np.abs(a[:, unstriped(n2)] - a) + 0.5))
    d_k2 = unpack_weight(d_words, d_scales)[np.arange(K)[:, None], runs(k2, K)]
    x_two = unpack_weight(x_words, x_scales)[:, unstriped(two)]
    b = 0.0625 * (d_k2.T @ x_two)
    z2 = f64(gm) * (np.abs(b - b[:, unstriped(n4)] - f64(tab)[:, unstriped(n3)]))
    h = unpack_weight(w1_words, w1_scales).T @ mxq(z, 0, "e4m3") + unpack_weight(w2_words, w2_scales).T @ mxq(z2, 0, "e4m3")
    out_0 = 0.75 * (h * h[:, unstriped(n5)] + h[:, unstriped(n6)] * h[:, unstriped(n7)])
    return (out_0,) + planes(out_0)

@@ -1,0 +1,223 @@
+from contextlib import ExitStack
+
+import concourse.mybir as mybir
+
+K, T, S, N, G, H, J = 512, 1024, 256, 512, 2048, 512, 512
+FLOPS = 2 * (2 * K * H * S) + 2 * (2 * H * N * S)
+
+F32 = mybir.dt.float32
+BF16 = mybir.dt.bfloat16
+I32 = mybir.dt.int32
+U32 = mybir.dt.uint32
+U16 = mybir.dt.uint16
+U8 = mybir.dt.uint8
+FP8X4 = mybir.dt.float8_e4m3fn_x4
+ALU = mybir.AluOpType
+ACT = mybir.ActivationFunctionType
+
+P = 128
+PACK = 4
+SPARE = 8
+
+
+def tile_picked_pqjfrackindddot_none_po_kernel(
+    tc, x_words, x_scales, d_words, d_scales, tab, gn, gm, w1_words, w1_scales, w2_words, w2_scales,
+    offs, k1, two, k2, n1, n2, n3, n4, n5, n6, n7, out_0, out_1, out_2,
+):
+    nc = tc.nc
+    with ExitStack() as ctx:
+        lists = ctx.enter_context(tc.tile_pool(name="lists", bufs=1))
+        keep = ctx.enter_context(tc.tile_pool(name="keep", bufs=1))
+        psum = ctx.enter_context(tc.psum_pool(name="psum", bufs=1))
+
+        def load_list(src, name):
+            tile = lists.tile(list(src.shape), U16, name=name)
+            nc.sync.dma_start(tile[:], src)
+            return tile
+
+        def words_in_hbm(src):
+            return src[0].rearrange("p n r -> p (n r)").bitcast(I32)
+
+        def load_words(src, name, tag=""):
+            tile = keep.tile([P, src.shape[2]], I32, name=name, tag=tag, align_bytes=64)
+            nc.sync.dma_start(tile[:], words_in_hbm(src))
+            return tile
+
+        def zeroed_bytes(width, name, engine, tag=""):
+            tile = keep.tile([P, width], U8, name=name, tag=tag, align_bytes=64)
+            engine.memset(tile[:].bitcast(I32), 0)
+            return tile
+
+        def load_scale_rows(tile, src, first, queue):
+            for q in range(4):
+                queue.dma_start(tile[32 * q + first : 32 * q + first + 4, :].bitcast(I32), src[0, 4 * q : 4 * q + 4, :].bitcast(I32))
+
+        def deal(src, dtype, name, tag):
+            tile = keep.tile([P, H], dtype, name=name, tag=tag, align_bytes=64)
+            nc.vector.tensor_copy(tile[:].rearrange("p (t m) -> p m t", t=PACK), src.rearrange("p (m t) -> p m t", t=PACK))
+            return tile
+
+        def gather_words(window, offsets, name):
+            tile = keep.tile([P, 16 * offsets.shape[1]], I32, name=name, align_bytes=64)
+            nc.vector.tensor_copy(tile[:].bitcast(U32), window[:].bitcast(U32).indirect(offsets[:]))
+            return tile
+
+        def gather_bytes(window, offsets, name):
+            tile = keep.tile([P, 16 * offsets.shape[1]], U8, name=name, align_bytes=64)
+            nc.vector.tensor_copy(tile[:], window[:].indirect(offsets[:]))
+            return tile
+
+        def window(name):
+            tile = keep.tile([P, S + SPARE], F32, name=name)
+            nc.gpsimd.memset(tile[:, S:], 0.0)
+            return tile
+
+        def rows(name):
+            return keep.tile([P, PACK, S], F32, name=name)
+
+        def fetch(out, src, offsets, scale=1.0):
+            nc.scalar.activation(out, src[:].indirect(offsets[:]), ACT.Copy, scale=scale)
+
+        def by_lines(ap):
+            return ap.rearrange("p t (c i) -> p c t i", i=4)
+
+        def woven(tile):
+            return tile[:].rearrange("p (c i t) -> p c t i", i=4, t=PACK)
+
+        def quantise(values, name):
+            codes = keep.tile([P, S], I32, name=name + "_codes", align_bytes=64)
+            plane = keep.tile([P, S], U8, name=name + "_plane", align_bytes=64)
+            nc.vector.quantize_mx(out=codes[:].bitcast(FP8X4), scales=plane[:], in_=values[:])
+            return codes, plane
+
+        d_sc = zeroed_bytes(G, "d_sc", nc.gpsimd, tag="d_sc")
+        x_sc = zeroed_bytes(T, "x_sc", nc.vector, tag="x_sc")
+        nc.scalar.dma_start(d_sc[0:P:8, :].bitcast(I32), d_scales[0].bitcast(I32))
+        nc.scalar.dma_start(x_sc[0:P:8, :].bitcast(I32), x_scales[0].bitcast(I32))
+        k1_l = load_list(k1, "k1_l")
+        k2_l = load_list(k2, "k2_l")
+        n3_l = load_list(n3, "n3_l")
+        tab_rows = tab.rearrange("(p t) j -> p t j", t=PACK)
+        kinds = rows("kinds")
+
+        def fetch_kinds(t):
+            tab_t = keep.tile([P, J], F32, name="tab%d" % t)
+            nc.sync.dma_start(tab_t[:], tab_rows[:, t, :])
+            fetch(kinds[:, t, :], tab_t, n3_l)
+
+        fetch_kinds(0)
+        offs_l = load_list(offs, "offs_l")
+        two_l = load_list(two, "two_l")
+        n2_l = load_list(n2, "n2_l")
+        n1_l = load_list(n1, "n1_l")
+        n4_l = load_list(n4, "n4_l")
+        gn_t = keep.tile([P, PACK], F32, name="gn_t")
+        nc.sync.dma_start(gn_t[:], gn.rearrange("(p t) o -> p (t o)", t=PACK))
+        fetch_kinds(1)
+        x_w = load_words(x_words, "x_w")
+        d_w = load_words(d_words, "d_w")
+        fetch_kinds(2)
+
+        picked = keep.tile([P, 2 * (H + S)], U8, name="picked", tag="picked", align_bytes=64)
+        col = 0
+        for table, offsets, width in ((d_sc, k1_l, H), (d_sc, k2_l, H), (x_sc, offs_l, S), (x_sc, two_l, S)):
+            nc.vector.tensor_copy(picked[:, col : col + width], table[:].indirect(offsets[:]))
+            col = col + width
+        dealt = keep.tile([P, 2 * (H + S)], U8, name="dealt", align_bytes=64)
+        nc.vector.tensor_copy(dealt[:, : 2 * H].rearrange("p (l t m) -> p l m t", l=2, t=PACK),
+                              picked[:, : 2 * H].rearrange("p (l m t) -> p l m t", l=2, t=PACK))
+        nc.vector.tensor_copy(dealt[:, 2 * H :].bitcast(I32), picked[:, 2 * H :].bitcast(I32))
+        placed = zeroed_bytes(2 * (H + S), "placed", nc.gpsimd, tag="placed")
+        for s in range(4):
+            nc.scalar.dma_start(placed[s:P:32, :].bitcast(I32), dealt[8 * s : P : 32, :].bitcast(I32))
+        fetch_kinds(3)
+
+        def coded_layer(which, k_l, x_l, name):
+            xw = gather_words(x_w, x_l, name + "_xw")
+            dw = deal(gather_words(d_w, k_l, name + "_dw_picked")[:], I32, name + "_dw", tag=name + "_dw")
+            ds = placed[:, H * which : H * (which + 1)]
+            xs = placed[:, 2 * H + S * which : 2 * H + S * (which + 1)]
+            banks = []
+            for t in range(PACK):
+                bank = psum.tile([P, S], F32, name=name + "_bank%d" % t, tag="bank%d" % (PACK * which + t))
+                cols = slice(P * t, P * (t + 1))
+                nc.tensor.matmul_mx(out=bank[:], lhsT=dw[:, cols].bitcast(FP8X4), lhsT_scale=ds[:, cols],
+                                    rhs=xw[:].bitcast(FP8X4), rhs_scale=xs, start=True, stop=True)
+                banks.append(bank)
+            return banks
+
+        a_banks = coded_layer(0, k1_l, offs_l, "a")
+        b_banks = coded_layer(1, k2_l, two_l, "b")
+
+        w1_in = load_words(w1_words, "w1_in", tag="d_sc")
+        w2_in = load_words(w2_words, "w2_in", tag="x_sc")
+        gm_t = keep.tile([P, PACK], F32, name="gm_t")
+        nc.sync.dma_start(gm_t[:], gm.rearrange("(p t) o -> p (t o)", t=PACK))
+        w_sc_in = zeroed_bytes(N, "w_sc_in", nc.gpsimd, tag="picked")
+        load_scale_rows(w_sc_in, w1_scales, 0, nc.sync)
+        load_scale_rows(w_sc_in, w2_scales, 4, nc.sync)
+        n7_l = load_list(n7, "n7_l")
+        n5_l = load_list(n5, "n5_l")
+        n6_l = load_list(n6, "n6_l")
+
+        at_n1, at_n2, numer, diff, size, root, factor = [rows(n) for n in ("at_n1", "at_n2", "numer", "diff", "size", "root", "factor")]
+        at_n4, less_kind, inner, size2 = [rows(n) for n in ("at_n4", "less_kind", "inner", "size2")]
+        for t in range(PACK):
+            a_t = window("a%d" % t)
+            nc.scalar.activation(a_t[:, :S], a_banks[t][:], ACT.Copy)
+            fetch(at_n2[:, t, :], a_t, n2_l)
+            fetch(at_n1[:, t, :], a_t, n1_l)
+            nc.vector.tensor_tensor(diff[:, t, :], at_n2[:, t, :], a_banks[t][:], ALU.subtract)
+            nc.vector.tensor_tensor(numer[:, t, :], a_banks[t][:], at_n1[:, t, :], ALU.subtract)
+        for t in range(PACK):
+            nc.vector.scalar_tensor_tensor(less_kind[:, t, :], b_banks[t][:], 0.0625, kinds[:, t, :], ALU.mult, ALU.subtract)
+        w1_w = deal(w1_in[:], I32, "w1_w", "a_dw")
+        w2_w = deal(w2_in[:], I32, "w2_w", "b_dw")
+        w_sc = deal(w_sc_in[:], U8, "w_sc", "placed")
+        for pair in (slice(0, 2), slice(2, 4)):
+            nc.scalar.activation(size[:, pair, :], diff[:, pair, :], ACT.Abs)
+            nc.scalar.activation(root[:, pair, :], size[:, pair, :], ACT.Abs_reciprocal_sqrt, bias=8.0)
+        for t in range(PACK):
+            nc.vector.scalar_tensor_tensor(factor[:, t, :], root[:, t, :], gn_t[:, t : t + 1], root[:, t, :], ALU.mult, ALU.mult)
+        z_bf = keep.tile([P, PACK * S], BF16, name="z_bf", align_bytes=64)
+        nc.vector.tensor_tensor(woven(z_bf), by_lines(numer[:]), by_lines(factor[:]), ALU.mult)
+        z_codes, z_plane = quantise(z_bf, "z")
+
+        for t in range(PACK):
+            b_t = window("b%d" % t)
+            nc.scalar.activation(b_t[:, :S], b_banks[t][:], ACT.Copy, scale=0.0625)
+            fetch(at_n4[:, t, :], b_t, n4_l)
+            nc.vector.tensor_tensor(inner[:, t, :], less_kind[:, t, :], at_n4[:, t, :], ALU.subtract)
+            nc.vector.scalar_tensor_tensor(size2[:, t, :], inner[:, t, :], -1.0, inner[:, t, :], ALU.mult, ALU.max)
+        z2_bf = keep.tile([P, PACK * S], BF16, name="z2_bf", align_bytes=64)
+        gm_wide = gm_t[:].unsqueeze(1).unsqueeze(3).to_broadcast([P, S // 4, PACK, 4])
+        nc.vector.tensor_tensor(woven(z2_bf), by_lines(size2[:]), gm_wide, ALU.mult)
+        z2_codes, z2_plane = quantise(z2_bf, "z2")
+
+        h_banks = [psum.tile([P, S], F32, name="h_bank%d" % t, tag="bank%d" % t) for t in range(PACK)]
+        for w_w, first, codes, plane in ((w1_w, 0, z_codes, z_plane), (w2_w, 4, z2_codes, z2_plane)):
+            for t in range(PACK):
+                cols = slice(P * t, P * (t + 1))
+                nc.tensor.matmul_mx(out=h_banks[t][:], lhsT=w_w[:, cols].bitcast(FP8X4), lhsT_scale=w_sc[first:P, cols],
+                                    rhs=codes[:].bitcast(FP8X4), rhs_scale=plane[:], start=(first == 0), stop=(first == 4))
+
+        at_n5, at_n7, left, right, result = [rows(n) for n in ("at_n5", "at_n7", "left", "right", "result")]
+        h_rows = [window("h%d" % t) for t in range(PACK)]
+        for t in range(PACK - 1):
+            nc.vector.tensor_copy(h_rows[t][:, :S], h_banks[t][:])
+        out_rows = out_0.rearrange("(p t) j -> p t j", t=PACK)
+        for t in range(PACK):
+            if t == PACK - 1:
+                nc.scalar.activation(h_rows[t][:, :S], h_banks[t][:], ACT.Copy)
+            fetch(at_n7[:, t, :], h_rows[t], n7_l)
+            fetch(at_n5[:, t, :], h_rows[t], n5_l)
+            nc.vector.tensor_tensor(right[:, t, :], h_rows[t][:].indirect(n6_l[:]), at_n7[:, t, :], ALU.mult)
+            nc.vector.scalar_tensor_tensor(left[:, t, :], h_banks[t][:], 0.75, at_n5[:, t, :], ALU.mult, ALU.mult)
+            nc.vector.scalar_tensor_tensor(result[:, t, :], right[:, t, :], 0.75, left[:, t, :], ALU.mult, ALU.add)
+            nc.sync.dma_start(out_rows[:, t, :], result[:, t, :])
+        y_bf = keep.tile([P, PACK * S], BF16, name="y_bf", align_bytes=64)
+        nc.vector.tensor_copy(woven(y_bf), by_lines(result[:]))
+        y_codes, y_plane = quantise(y_bf, "y")
+        nc.sync.dma_start(words_in_hbm(out_1), y_codes[:])
+        for q in range(4):
+            nc.scalar.dma_start(out_2[0, 4 * q : 4 * q + 4, :].bitcast(I32), y_plane[32 * q : 32 * q + 4, :].bitcast(I32))

@@ -17,7 +17,11 @@ ACT = mybir.ActivationFunctionType
 
 P = 128
 PACK = 4
+HALF = S // 2
 SPARE = 8
+WIDE_SPARE = 96
+N2_ON_SCALAR = 2
+H_ON_VECTOR = 4
 
 
 def tile_picked_pqjfrackindddot_none_po_kernel(
@@ -28,6 +32,8 @@ def tile_picked_pqjfrackindddot_none_po_kernel(
     with ExitStack() as ctx:
         lists = ctx.enter_context(tc.tile_pool(name="lists", bufs=1))
         keep = ctx.enter_context(tc.tile_pool(name="keep", bufs=1))
+        stage = ctx.enter_context(tc.tile_pool(name="stage", bufs=1))
+        late = ctx.enter_context(tc.tile_pool(name="late", bufs=1))
         psum = ctx.enter_context(tc.psum_pool(name="psum", bufs=1))
 
         def load_list(src, name):
@@ -57,8 +63,8 @@ def tile_picked_pqjfrackindddot_none_po_kernel(
             nc.vector.tensor_copy(tile[:].rearrange("p (t m) -> p m t", t=PACK), src.rearrange("p (m t) -> p m t", t=PACK))
             return tile
 
-        def gather_words(window, offsets, name):
-            tile = keep.tile([P, 16 * offsets.shape[1]], I32, name=name, align_bytes=64)
+        def gather_words(window, offsets, name, at):
+            tile = stage.tile([P, 16 * offsets.shape[1]], I32, name=name, align_bytes=64, offset=at)
             nc.vector.tensor_copy(tile[:].bitcast(U32), window[:].bitcast(U32).indirect(offsets[:]))
             return tile
 
@@ -67,8 +73,8 @@ def tile_picked_pqjfrackindddot_none_po_kernel(
             nc.vector.tensor_copy(tile[:], window[:].indirect(offsets[:]))
             return tile
 
-        def window(name):
-            tile = keep.tile([P, S + SPARE], F32, name=name)
+        def window(name, spare=SPARE):
+            tile = keep.tile([P, S + spare], F32, name=name)
             nc.gpsimd.memset(tile[:, S:], 0.0)
             return tile
 
@@ -81,8 +87,8 @@ def tile_picked_pqjfrackindddot_none_po_kernel(
         def by_lines(ap):
             return ap.rearrange("p t (c i) -> p c t i", i=4)
 
-        def woven(tile):
-            return tile[:].rearrange("p (c i t) -> p c t i", i=4, t=PACK)
+        def woven(ap):
+            return ap.rearrange("p (c i t) -> p c t i", i=4, t=PACK)
 
         def quantise(values, name):
             codes = keep.tile([P, S], I32, name=name + "_codes", align_bytes=64)
@@ -90,51 +96,47 @@ def tile_picked_pqjfrackindddot_none_po_kernel(
             nc.vector.quantize_mx(out=codes[:].bitcast(FP8X4), scales=plane[:], in_=values[:])
             return codes, plane
 
-        d_sc = zeroed_bytes(G, "d_sc", nc.gpsimd, tag="d_sc")
-        x_sc = zeroed_bytes(T, "x_sc", nc.vector, tag="x_sc")
-        nc.scalar.dma_start(d_sc[0:P:8, :].bitcast(I32), d_scales[0].bitcast(I32))
-        nc.scalar.dma_start(x_sc[0:P:8, :].bitcast(I32), x_scales[0].bitcast(I32))
+        d_sc = keep.tile([P, G], U8, name="d_sc", align_bytes=64)
+        nc.gpsimd.memset(d_sc[:].bitcast(I32), 0)
+        x_sc = keep.tile([P, T], U8, name="x_sc", align_bytes=64)
+        nc.gpsimd.memset(x_sc[:].bitcast(I32), 0)
+        nc.sync.dma_start(d_sc[0:P:8, :].bitcast(I32), d_scales[0].bitcast(I32))
+        nc.sync.dma_start(x_sc[0:P:8, :].bitcast(I32), x_scales[0].bitcast(I32))
+        a_rows = [window("a%d" % t, SPARE if t < N2_ON_SCALAR else WIDE_SPARE) for t in range(PACK)]
+        unread = keep.tile([P, 1], F32, name="unread")
+        nc.scalar.activation(unread[:], a_rows[0][:, S : S + 1], ACT.Abs_reciprocal_sqrt, bias=8.0)
         k1_l = load_list(k1, "k1_l")
         k2_l = load_list(k2, "k2_l")
+        offs_l = load_list(offs, "offs_l")
+        two_l = load_list(two, "two_l")
+        x_w = load_words(x_words, "x_w")
+        d_w = load_words(d_words, "d_w")
         n3_l = load_list(n3, "n3_l")
         tab_rows = tab.rearrange("(p t) j -> p t j", t=PACK)
         kinds = rows("kinds")
-
-        def fetch_kinds(t):
+        for t in range(PACK):
             tab_t = keep.tile([P, J], F32, name="tab%d" % t)
             nc.sync.dma_start(tab_t[:], tab_rows[:, t, :])
             fetch(kinds[:, t, :], tab_t, n3_l)
-
-        fetch_kinds(0)
-        offs_l = load_list(offs, "offs_l")
-        two_l = load_list(two, "two_l")
         n2_l = load_list(n2, "n2_l")
-        n1_l = load_list(n1, "n1_l")
-        n4_l = load_list(n4, "n4_l")
-        gn_t = keep.tile([P, PACK], F32, name="gn_t")
-        nc.sync.dma_start(gn_t[:], gn.rearrange("(p t) o -> p (t o)", t=PACK))
-        fetch_kinds(1)
-        x_w = load_words(x_words, "x_w")
-        d_w = load_words(d_words, "d_w")
-        fetch_kinds(2)
 
-        picked = keep.tile([P, 2 * (H + S)], U8, name="picked", tag="picked", align_bytes=64)
-        col = 0
-        for table, offsets, width in ((d_sc, k1_l, H), (d_sc, k2_l, H), (x_sc, offs_l, S), (x_sc, two_l, S)):
-            nc.vector.tensor_copy(picked[:, col : col + width], table[:].indirect(offsets[:]))
-            col = col + width
+        picked = keep.tile([P, 2 * (H + S)], U8, name="picked", align_bytes=64)
         dealt = keep.tile([P, 2 * (H + S)], U8, name="dealt", align_bytes=64)
-        nc.vector.tensor_copy(dealt[:, : 2 * H].rearrange("p (l t m) -> p l m t", l=2, t=PACK),
-                              picked[:, : 2 * H].rearrange("p (l m t) -> p l m t", l=2, t=PACK))
+        nc.vector.tensor_copy(picked[:, :H], d_sc[:].indirect(k1_l[:]))
+        nc.vector.tensor_copy(picked[:, H : 2 * H], d_sc[:].indirect(k2_l[:]))
+        nc.vector.tensor_copy(picked[:, 2 * H : 2 * H + S], x_sc[:].indirect(offs_l[:]))
+        nc.vector.tensor_copy(picked[:, 2 * H + S :], x_sc[:].indirect(two_l[:]))
+        for cols in (slice(0, H), slice(H, 2 * H)):
+            nc.vector.tensor_copy(dealt[:, cols].rearrange("p (t m) -> p m t", t=PACK), picked[:, cols].rearrange("p (m t) -> p m t", t=PACK))
         nc.vector.tensor_copy(dealt[:, 2 * H :].bitcast(I32), picked[:, 2 * H :].bitcast(I32))
-        placed = zeroed_bytes(2 * (H + S), "placed", nc.gpsimd, tag="placed")
+        placed = zeroed_bytes(2 * (H + S), "placed", nc.gpsimd)
         for s in range(4):
-            nc.scalar.dma_start(placed[s:P:32, :].bitcast(I32), dealt[8 * s : P : 32, :].bitcast(I32))
-        fetch_kinds(3)
+            nc.sync.dma_start(placed[s:P:32, :].bitcast(I32), dealt[8 * s : P : 32, :].bitcast(I32))
 
-        def coded_layer(which, k_l, x_l, name):
-            xw = gather_words(x_w, x_l, name + "_xw")
-            dw = deal(gather_words(d_w, k_l, name + "_dw_picked")[:], I32, name + "_dw", tag=name + "_dw")
+        def coded_layer(which, k_l, x_l, name, d_at, x_at):
+            picked_words = gather_words(d_w, k_l, name + "_dw_picked", d_at)
+            xw = gather_words(x_w, x_l, name + "_xw", x_at)
+            dw = deal(picked_words[:], I32, name + "_dw", tag=name + "_dw")
             ds = placed[:, H * which : H * (which + 1)]
             xs = placed[:, 2 * H + S * which : 2 * H + S * (which + 1)]
             banks = []
@@ -146,78 +148,114 @@ def tile_picked_pqjfrackindddot_none_po_kernel(
                 banks.append(bank)
             return banks
 
-        a_banks = coded_layer(0, k1_l, offs_l, "a")
-        b_banks = coded_layer(1, k2_l, two_l, "b")
+        a_banks = coded_layer(0, k1_l, offs_l, "a", 1024, 3072)
+        b_banks = coded_layer(1, k2_l, two_l, "b", 0, 2048)
 
-        w1_in = load_words(w1_words, "w1_in", tag="d_sc")
-        w2_in = load_words(w2_words, "w2_in", tag="x_sc")
+        w1_in = load_words(w1_words, "w1_in")
+        w2_in = load_words(w2_words, "w2_in")
+        n4_l = load_list(n4, "n4_l")
         gm_t = keep.tile([P, PACK], F32, name="gm_t")
         nc.sync.dma_start(gm_t[:], gm.rearrange("(p t) o -> p (t o)", t=PACK))
-        w_sc_in = zeroed_bytes(N, "w_sc_in", nc.gpsimd, tag="picked")
+        gn_t = keep.tile([P, PACK], F32, name="gn_t")
+        nc.sync.dma_start(gn_t[:], gn.rearrange("(p t) o -> p (t o)", t=PACK))
+        n1_l = load_list(n1, "n1_l")
+        w_sc_in = zeroed_bytes(N, "w_sc_in", nc.gpsimd)
         load_scale_rows(w_sc_in, w1_scales, 0, nc.sync)
         load_scale_rows(w_sc_in, w2_scales, 4, nc.sync)
         n7_l = load_list(n7, "n7_l")
         n5_l = load_list(n5, "n5_l")
         n6_l = load_list(n6, "n6_l")
 
-        at_n1, at_n2, numer, diff, size, root, factor = [rows(n) for n in ("at_n1", "at_n2", "numer", "diff", "size", "root", "factor")]
-        at_n4, less_kind, inner, size2 = [rows(n) for n in ("at_n4", "less_kind", "inner", "size2")]
+        at_n2, diff, size, root, factor = [rows(n) for n in ("at_n2", "diff", "size", "root", "factor")]
+        at_n4, less_kind, size2 = [rows(n) for n in ("at_n4", "less_kind", "size2")]
+        inner = late.tile([P, PACK, S], F32, name="inner", offset=0)
+        pairs = (slice(0, 2), slice(2, 4))
         for t in range(PACK):
-            a_t = window("a%d" % t)
-            nc.scalar.activation(a_t[:, :S], a_banks[t][:], ACT.Copy)
-            fetch(at_n2[:, t, :], a_t, n2_l)
-            fetch(at_n1[:, t, :], a_t, n1_l)
+            nc.scalar.activation(a_rows[t][:, :S], a_banks[t][:], ACT.Copy)
+        for t in range(PACK):
+            if t < N2_ON_SCALAR:
+                fetch(at_n2[:, t, :], a_rows[t], n2_l)
+            else:
+                nc.vector.tensor_copy(at_n2[:, t, :], a_rows[t][:].indirect(n2_l[:]))
+        b_rows = [window("b%d" % t) for t in range(PACK)]
+        for t in range(PACK):
+            nc.scalar.activation(b_rows[t][:, :S], b_banks[t][:], ACT.Copy, scale=0.0625)
+        for t in range(PACK):
             nc.vector.tensor_tensor(diff[:, t, :], at_n2[:, t, :], a_banks[t][:], ALU.subtract)
-            nc.vector.tensor_tensor(numer[:, t, :], a_banks[t][:], at_n1[:, t, :], ALU.subtract)
+        for pair in pairs:
+            nc.vector.scalar_tensor_tensor(size[:, pair, :], diff[:, pair, :], -1.0, diff[:, pair, :], ALU.mult, ALU.max)
         for t in range(PACK):
             nc.vector.scalar_tensor_tensor(less_kind[:, t, :], b_banks[t][:], 0.0625, kinds[:, t, :], ALU.mult, ALU.subtract)
-        w1_w = deal(w1_in[:], I32, "w1_w", "a_dw")
-        w2_w = deal(w2_in[:], I32, "w2_w", "b_dw")
-        w_sc = deal(w_sc_in[:], U8, "w_sc", "placed")
-        for pair in (slice(0, 2), slice(2, 4)):
-            nc.scalar.activation(size[:, pair, :], diff[:, pair, :], ACT.Abs)
+        for t in range(PACK):
+            fetch(at_n4[:, t, :], b_rows[t], n4_l)
+        for pair in pairs:
+            nc.vector.tensor_tensor(inner[:, pair, :], less_kind[:, pair, :], at_n4[:, pair, :], ALU.subtract)
+        for pair in pairs:
             nc.scalar.activation(root[:, pair, :], size[:, pair, :], ACT.Abs_reciprocal_sqrt, bias=8.0)
+        for pair in pairs:
+            nc.scalar.activation(size2[:, pair, :], inner[:, pair, :], ACT.Abs)
+        w1_w = deal(w1_in[:], I32, "w1_w", "w1_w")
+        w2_w = deal(w2_in[:], I32, "w2_w", "w2_w")
+        w_sc = keep.tile([P, N], U8, name="w_sc", align_bytes=64)
+        nc.gpsimd.tensor_copy(w_sc[:].rearrange("p (t m) -> p t m", t=PACK), w_sc_in[:].rearrange("p (m t) -> p t m", t=PACK))
         for t in range(PACK):
             nc.vector.scalar_tensor_tensor(factor[:, t, :], root[:, t, :], gn_t[:, t : t + 1], root[:, t, :], ALU.mult, ALU.mult)
-        z_bf = keep.tile([P, PACK * S], BF16, name="z_bf", align_bytes=64)
-        nc.vector.tensor_tensor(woven(z_bf), by_lines(numer[:]), by_lines(factor[:]), ALU.mult)
-        z_codes, z_plane = quantise(z_bf, "z")
-
-        for t in range(PACK):
-            b_t = window("b%d" % t)
-            nc.scalar.activation(b_t[:, :S], b_banks[t][:], ACT.Copy, scale=0.0625)
-            fetch(at_n4[:, t, :], b_t, n4_l)
-            nc.vector.tensor_tensor(inner[:, t, :], less_kind[:, t, :], at_n4[:, t, :], ALU.subtract)
-            nc.vector.scalar_tensor_tensor(size2[:, t, :], inner[:, t, :], -1.0, inner[:, t, :], ALU.mult, ALU.max)
         z2_bf = keep.tile([P, PACK * S], BF16, name="z2_bf", align_bytes=64)
         gm_wide = gm_t[:].unsqueeze(1).unsqueeze(3).to_broadcast([P, S // 4, PACK, 4])
-        nc.vector.tensor_tensor(woven(z2_bf), by_lines(size2[:]), gm_wide, ALU.mult)
+        nc.vector.tensor_tensor(woven(z2_bf[:]), by_lines(size2[:]), gm_wide, ALU.mult)
         z2_codes, z2_plane = quantise(z2_bf, "z2")
+        h_banks = [psum.tile([P, S], F32, name="h_bank%d" % t, tag="bank%d" % (PACK + t)) for t in range(PACK)]
 
-        h_banks = [psum.tile([P, S], F32, name="h_bank%d" % t, tag="bank%d" % t) for t in range(PACK)]
-        for w_w, first, codes, plane in ((w1_w, 0, z_codes, z_plane), (w2_w, 4, z2_codes, z2_plane)):
+        def product(w_w, first, codes, plane, places, start, stop):
             for t in range(PACK):
                 cols = slice(P * t, P * (t + 1))
-                nc.tensor.matmul_mx(out=h_banks[t][:], lhsT=w_w[:, cols].bitcast(FP8X4), lhsT_scale=w_sc[first:P, cols],
-                                    rhs=codes[:].bitcast(FP8X4), rhs_scale=plane[:], start=(first == 0), stop=(first == 4))
+                nc.tensor.matmul_mx(out=h_banks[t][:, places], lhsT=w_w[:, cols].bitcast(FP8X4), lhsT_scale=w_sc[first:P, cols],
+                                    rhs=codes[:, places].bitcast(FP8X4), rhs_scale=plane[:, places], start=start, stop=stop)
+
+        product(w2_w, 4, z2_codes, z2_plane, slice(0, S), True, False)
+        z_bf = keep.tile([P, PACK * S], BF16, name="z_bf", align_bytes=64)
+        z_codes = keep.tile([P, S], I32, name="z_codes", align_bytes=64)
+        z_plane = keep.tile([P, S], U8, name="z_plane", align_bytes=64)
+        for half in range(2):
+            places = slice(HALF * half, HALF * (half + 1))
+            entries = slice(HALF // 16 * half, HALF // 16 * (half + 1))
+            values = z_bf[:, PACK * HALF * half : PACK * HALF * (half + 1)]
+            at_n1 = late.tile([P, PACK, HALF], F32, name="at_n1_%d" % half, offset=4 * PACK * HALF * half)
+            numer = keep.tile([P, PACK, HALF], F32, name="numer%d" % half)
+            for t in range(PACK):
+                nc.scalar.activation(at_n1[:, t, :], a_rows[t][:].indirect(n1_l[:, entries]), ACT.Copy)
+                nc.vector.tensor_tensor(numer[:, t, :], a_banks[t][:, places], at_n1[:, t, :], ALU.subtract)
+            nc.vector.tensor_tensor(woven(values), by_lines(numer[:]), by_lines(factor[:, :, places]), ALU.mult)
+            nc.vector.quantize_mx(out=z_codes[:, places].bitcast(FP8X4), scales=z_plane[:, places], in_=values)
+            product(w1_w, 0, z_codes, z_plane, places, False, half == 1)
 
         at_n5, at_n7, left, right, result = [rows(n) for n in ("at_n5", "at_n7", "left", "right", "result")]
         h_rows = [window("h%d" % t) for t in range(PACK)]
-        for t in range(PACK - 1):
+        for t in range(H_ON_VECTOR):
             nc.vector.tensor_copy(h_rows[t][:, :S], h_banks[t][:])
         out_rows = out_0.rearrange("(p t) j -> p t j", t=PACK)
-        for t in range(PACK):
-            if t == PACK - 1:
-                nc.scalar.activation(h_rows[t][:, :S], h_banks[t][:], ACT.Copy)
-            fetch(at_n7[:, t, :], h_rows[t], n7_l)
-            fetch(at_n5[:, t, :], h_rows[t], n5_l)
-            nc.vector.tensor_tensor(right[:, t, :], h_rows[t][:].indirect(n6_l[:]), at_n7[:, t, :], ALU.mult)
-            nc.vector.scalar_tensor_tensor(left[:, t, :], h_banks[t][:], 0.75, at_n5[:, t, :], ALU.mult, ALU.mult)
-            nc.vector.scalar_tensor_tensor(result[:, t, :], right[:, t, :], 0.75, left[:, t, :], ALU.mult, ALU.add)
-            nc.sync.dma_start(out_rows[:, t, :], result[:, t, :])
         y_bf = keep.tile([P, PACK * S], BF16, name="y_bf", align_bytes=64)
-        nc.vector.tensor_copy(woven(y_bf), by_lines(result[:]))
-        y_codes, y_plane = quantise(y_bf, "y")
+        y_codes = keep.tile([P, S], I32, name="y_codes", align_bytes=64)
+        y_plane = keep.tile([P, S], U8, name="y_plane", align_bytes=64)
+        last = PACK - 1
+        for t in range(PACK):
+            fetch(at_n7[:, t, :], h_rows[t], n7_l)
+            nc.vector.tensor_tensor(right[:, t, :], h_rows[t][:].indirect(n6_l[:]), at_n7[:, t, :], ALU.mult)
+            if t < last:
+                fetch(at_n5[:, t, :], h_rows[t], n5_l)
+                nc.vector.scalar_tensor_tensor(left[:, t, :], h_banks[t][:], 0.75, at_n5[:, t, :], ALU.mult, ALU.mult)
+                nc.vector.scalar_tensor_tensor(result[:, t, :], right[:, t, :], 0.75, left[:, t, :], ALU.mult, ALU.add)
+                nc.sync.dma_start(out_rows[:, t, :], result[:, t, :])
+        fetch(at_n5[:, last, :], h_rows[last], n5_l)
+        nc.vector.scalar_tensor_tensor(left[:, last, :], h_banks[last][:], 0.75, at_n5[:, last, :], ALU.mult, ALU.mult)
+        halves = [slice(HALF * half, HALF * (half + 1)) for half in range(2)]
+        for places in halves:
+            nc.vector.scalar_tensor_tensor(result[:, last, places], right[:, last, places], 0.75, left[:, last, places], ALU.mult, ALU.add)
+        nc.sync.dma_start(out_rows[:, last, :], result[:, last, :])
+        for places in halves:
+            nc.vector.tensor_copy(woven(y_bf[:, PACK * places.start : PACK * places.stop]), by_lines(result[:, :, places]))
+        for places in halves:
+            nc.vector.quantize_mx(out=y_codes[:, places].bitcast(FP8X4), scales=y_plane[:, places], in_=y_bf[:, PACK * places.start : PACK * places.stop])
         nc.sync.dma_start(words_in_hbm(out_1), y_codes[:])
         for q in range(4):
             nc.scalar.dma_start(out_2[0, 4 * q : 4 * q + 4, :].bitcast(I32), y_plane[32 * q : 32 * q + 4, :].bitcast(I32))

@@ -96,19 +96,17 @@ def tile_picked_pqjfrackindddot_none_po_kernel(
             nc.vector.quantize_mx(out=codes[:].bitcast(FP8X4), scales=plane[:], in_=values[:])
             return codes, plane
 
-        d_sc = keep.tile([P, G], U8, name="d_sc", align_bytes=64)
-        nc.gpsimd.memset(d_sc[:].bitcast(I32), 0)
-        x_sc = keep.tile([P, T], U8, name="x_sc", align_bytes=64)
-        nc.gpsimd.memset(x_sc[:].bitcast(I32), 0)
-        nc.sync.dma_start(d_sc[0:P:8, :].bitcast(I32), d_scales[0].bitcast(I32))
+        x_sc = zeroed_bytes(T, "x_sc", nc.gpsimd)
+        d_sc = zeroed_bytes(G, "d_sc", nc.gpsimd)
+        offs_l = load_list(offs, "offs_l")
         nc.sync.dma_start(x_sc[0:P:8, :].bitcast(I32), x_scales[0].bitcast(I32))
+        two_l = load_list(two, "two_l")
+        k1_l = load_list(k1, "k1_l")
+        k2_l = load_list(k2, "k2_l")
+        nc.sync.dma_start(d_sc[0:P:8, :].bitcast(I32), d_scales[0].bitcast(I32))
         a_rows = [window("a%d" % t, SPARE if t < N2_ON_SCALAR else WIDE_SPARE) for t in range(PACK)]
         unread = keep.tile([P, 1], F32, name="unread")
         nc.scalar.activation(unread[:], a_rows[0][:, S : S + 1], ACT.Abs_reciprocal_sqrt, bias=8.0)
-        k1_l = load_list(k1, "k1_l")
-        k2_l = load_list(k2, "k2_l")
-        offs_l = load_list(offs, "offs_l")
-        two_l = load_list(two, "two_l")
         x_w = load_words(x_words, "x_w")
         d_w = load_words(d_words, "d_w")
         n3_l = load_list(n3, "n3_l")
@@ -122,13 +120,13 @@ def tile_picked_pqjfrackindddot_none_po_kernel(
 
         picked = keep.tile([P, 2 * (H + S)], U8, name="picked", align_bytes=64)
         dealt = keep.tile([P, 2 * (H + S)], U8, name="dealt", align_bytes=64)
-        nc.vector.tensor_copy(picked[:, :H], d_sc[:].indirect(k1_l[:]))
-        nc.vector.tensor_copy(picked[:, H : 2 * H], d_sc[:].indirect(k2_l[:]))
         nc.vector.tensor_copy(picked[:, 2 * H : 2 * H + S], x_sc[:].indirect(offs_l[:]))
         nc.vector.tensor_copy(picked[:, 2 * H + S :], x_sc[:].indirect(two_l[:]))
+        nc.vector.tensor_copy(picked[:, :H], d_sc[:].indirect(k1_l[:]))
+        nc.vector.tensor_copy(picked[:, H : 2 * H], d_sc[:].indirect(k2_l[:]))
+        nc.vector.tensor_copy(dealt[:, 2 * H :].bitcast(I32), picked[:, 2 * H :].bitcast(I32))
         for cols in (slice(0, H), slice(H, 2 * H)):
             nc.vector.tensor_copy(dealt[:, cols].rearrange("p (t m) -> p m t", t=PACK), picked[:, cols].rearrange("p (m t) -> p m t", t=PACK))
-        nc.vector.tensor_copy(dealt[:, 2 * H :].bitcast(I32), picked[:, 2 * H :].bitcast(I32))
         placed = zeroed_bytes(2 * (H + S), "placed", nc.gpsimd)
         for s in range(4):
             nc.sync.dma_start(placed[s:P:32, :].bitcast(I32), dealt[8 * s : P : 32, :].bitcast(I32))
@@ -167,8 +165,8 @@ def tile_picked_pqjfrackindddot_none_po_kernel(
         n6_l = load_list(n6, "n6_l")
 
         at_n2, diff, size, root, factor = [rows(n) for n in ("at_n2", "diff", "size", "root", "factor")]
-        at_n4, less_kind, size2 = [rows(n) for n in ("at_n4", "less_kind", "size2")]
-        inner = late.tile([P, PACK, S], F32, name="inner", offset=0)
+        inner, less_kind, size2 = [rows(n) for n in ("inner", "less_kind", "size2")]
+        at_n4 = late.tile([P, PACK, S], F32, name="at_n4", offset=0)
         pairs = (slice(0, 2), slice(2, 4))
         for t in range(PACK):
             nc.scalar.activation(a_rows[t][:, :S], a_banks[t][:], ACT.Copy)
@@ -258,4 +256,4 @@ def tile_picked_pqjfrackindddot_none_po_kernel(
             nc.vector.quantize_mx(out=y_codes[:, places].bitcast(FP8X4), scales=y_plane[:, places], in_=y_bf[:, PACK * places.start : PACK * places.stop])
         nc.sync.dma_start(words_in_hbm(out_1), y_codes[:])
         for q in range(4):
-            nc.scalar.dma_start(out_2[0, 4 * q : 4 * q + 4, :].bitcast(I32), y_plane[32 * q : 32 * q + 4, :].bitcast(I32))
+            (nc.scalar if q < 2 else nc.sync).dma_start(out_2[0, 4 * q : 4 * q + 4, :].bitcast(I32), y_plane[32 * q : 32 * q + 4, :].bitcast(I32))

@@ -18,10 +18,9 @@ ACT = mybir.ActivationFunctionType
 P = 128
 PACK = 4
 HALF = S // 2
-SPARE = 8
-WIDE_SPARE = 96
+SCALAR_SPARE = 8
+VECTOR_SPARE = 96
 N2_ON_SCALAR = 2
-H_ON_VECTOR = 4
 
 
 def tile_picked_pqjfrackindddot_none_po_kernel(
@@ -32,8 +31,7 @@ def tile_picked_pqjfrackindddot_none_po_kernel(
     with ExitStack() as ctx:
         lists = ctx.enter_context(tc.tile_pool(name="lists", bufs=1))
         keep = ctx.enter_context(tc.tile_pool(name="keep", bufs=1))
-        stage = ctx.enter_context(tc.tile_pool(name="stage", bufs=1))
-        late = ctx.enter_context(tc.tile_pool(name="late", bufs=1))
+        shared = ctx.enter_context(tc.tile_pool(name="shared", bufs=1))
         psum = ctx.enter_context(tc.psum_pool(name="psum", bufs=1))
 
         def load_list(src, name):
@@ -44,216 +42,226 @@ def tile_picked_pqjfrackindddot_none_po_kernel(
         def words_in_hbm(src):
             return src[0].rearrange("p n r -> p (n r)").bitcast(I32)
 
-        def load_words(src, name, tag=""):
-            tile = keep.tile([P, src.shape[2]], I32, name=name, tag=tag, align_bytes=64)
+        def load_words(src, name):
+            tile = keep.tile([P, src.shape[2]], I32, name=name, align_bytes=64)
             nc.sync.dma_start(tile[:], words_in_hbm(src))
             return tile
 
-        def zeroed_bytes(width, name, engine, tag=""):
-            tile = keep.tile([P, width], U8, name=name, tag=tag, align_bytes=64)
+        def load_gains(src, name):
+            tile = keep.tile([P, PACK], F32, name=name)
+            nc.sync.dma_start(tile[:], src.rearrange("(p t) o -> p (t o)", t=PACK))
+            return tile
+
+        def zeroed_bytes(width, name, engine):
+            tile = keep.tile([P, width], U8, name=name, align_bytes=64)
             engine.memset(tile[:].bitcast(I32), 0)
             return tile
 
-        def load_scale_rows(tile, src, first, queue):
-            for q in range(4):
-                queue.dma_start(tile[32 * q + first : 32 * q + first + 4, :].bitcast(I32), src[0, 4 * q : 4 * q + 4, :].bitcast(I32))
-
-        def deal(src, dtype, name, tag):
-            tile = keep.tile([P, H], dtype, name=name, tag=tag, align_bytes=64)
+        def deal(src, dtype, name):
+            tile = keep.tile([P, H], dtype, name=name, align_bytes=64)
             nc.vector.tensor_copy(tile[:].rearrange("p (t m) -> p m t", t=PACK), src.rearrange("p (m t) -> p m t", t=PACK))
             return tile
 
-        def gather_words(window, offsets, name, at):
-            tile = stage.tile([P, 16 * offsets.shape[1]], I32, name=name, align_bytes=64, offset=at)
-            nc.vector.tensor_copy(tile[:].bitcast(U32), window[:].bitcast(U32).indirect(offsets[:]))
+        def gather_words(table, offsets, name, tag):
+            tile = keep.tile([P, 16 * offsets.shape[1]], I32, name=name, tag=tag, align_bytes=64)
+            nc.vector.tensor_copy(tile[:].bitcast(U32), table[:].bitcast(U32).indirect(offsets[:]))
             return tile
 
-        def gather_bytes(window, offsets, name):
-            tile = keep.tile([P, 16 * offsets.shape[1]], U8, name=name, align_bytes=64)
-            nc.vector.tensor_copy(tile[:], window[:].indirect(offsets[:]))
-            return tile
-
-        def window(name, spare=SPARE):
+        def window(name, spare):
             tile = keep.tile([P, S + spare], F32, name=name)
-            nc.gpsimd.memset(tile[:, S:], 0.0)
+            nc.vector.memset(tile[:, S:], 0.0)
             return tile
 
-        def rows(name):
+        def row_tiles(name):
             return keep.tile([P, PACK, S], F32, name=name)
 
-        def fetch(out, src, offsets, scale=1.0):
-            nc.scalar.activation(out, src[:].indirect(offsets[:]), ACT.Copy, scale=scale)
+        def scalar_fetch(out, src, offsets):
+            nc.scalar.activation(out, src[:].indirect(offsets), ACT.Copy)
 
-        def by_lines(ap):
+        def in_fours(ap):
             return ap.rearrange("p t (c i) -> p c t i", i=4)
 
         def woven(ap):
             return ap.rearrange("p (c i t) -> p c t i", i=4, t=PACK)
 
-        def quantise(values, name):
+        def mx_tiles(name):
+            values = keep.tile([P, PACK * S], BF16, name=name + "_bf16", align_bytes=64)
             codes = keep.tile([P, S], I32, name=name + "_codes", align_bytes=64)
-            plane = keep.tile([P, S], U8, name=name + "_plane", align_bytes=64)
-            nc.vector.quantize_mx(out=codes[:].bitcast(FP8X4), scales=plane[:], in_=values[:])
-            return codes, plane
+            scales = keep.tile([P, S], U8, name=name + "_scales", align_bytes=64)
+            return values, codes, scales
 
-        x_sc = zeroed_bytes(T, "x_sc", nc.gpsimd)
-        d_sc = zeroed_bytes(G, "d_sc", nc.gpsimd)
+        def quantise(values, codes, scales, places):
+            nc.vector.quantize_mx(out=codes[:, places].bitcast(FP8X4), scales=scales[:, places],
+                                  in_=values[:, PACK * places.start : PACK * places.stop])
+
+        tiles = range(PACK)
+        pairs = (slice(0, 2), slice(2, 4))
+        halves = (slice(0, HALF), slice(HALF, S))
+        whole = slice(0, S)
+
+        x_bytes = zeroed_bytes(T, "x_bytes", nc.gpsimd)
+        d_bytes = zeroed_bytes(G, "d_bytes", nc.gpsimd)
         offs_l = load_list(offs, "offs_l")
-        nc.sync.dma_start(x_sc[0:P:8, :].bitcast(I32), x_scales[0].bitcast(I32))
+        nc.sync.dma_start(x_bytes[0:P:8, :].bitcast(I32), x_scales[0].bitcast(I32))
         two_l = load_list(two, "two_l")
         k1_l = load_list(k1, "k1_l")
         k2_l = load_list(k2, "k2_l")
-        nc.sync.dma_start(d_sc[0:P:8, :].bitcast(I32), d_scales[0].bitcast(I32))
-        a_rows = [window("a%d" % t, SPARE if t < N2_ON_SCALAR else WIDE_SPARE) for t in range(PACK)]
+        nc.sync.dma_start(d_bytes[0:P:8, :].bitcast(I32), d_scales[0].bitcast(I32))
+        a_rows = [window("a%d" % t, SCALAR_SPARE if t < N2_ON_SCALAR else VECTOR_SPARE) for t in tiles]
         unread = keep.tile([P, 1], F32, name="unread")
         nc.scalar.activation(unread[:], a_rows[0][:, S : S + 1], ACT.Abs_reciprocal_sqrt, bias=8.0)
         x_w = load_words(x_words, "x_w")
         d_w = load_words(d_words, "d_w")
         n3_l = load_list(n3, "n3_l")
         tab_rows = tab.rearrange("(p t) j -> p t j", t=PACK)
-        kinds = rows("kinds")
-        for t in range(PACK):
+        at_n3 = row_tiles("at_n3")
+
+        def fetch_kinds(t):
             tab_t = keep.tile([P, J], F32, name="tab%d" % t)
             nc.sync.dma_start(tab_t[:], tab_rows[:, t, :])
-            fetch(kinds[:, t, :], tab_t, n3_l)
+            scalar_fetch(at_n3[:, t, :], tab_t, n3_l[:])
+
+        for t in range(PACK - 1):
+            fetch_kinds(t)
+
+        picked = keep.tile([P, 2 * (H + S)], U8, name="picked", tag="picked", align_bytes=64)
+        nc.vector.tensor_copy(picked[:, 2 * H : 2 * H + S], x_bytes[:].indirect(offs_l[:]))
+        nc.vector.tensor_copy(picked[:, 2 * H + S :], x_bytes[:].indirect(two_l[:]))
+        nc.vector.tensor_copy(picked[:, :H], d_bytes[:].indirect(k1_l[:]))
+        nc.vector.tensor_copy(picked[:, H : 2 * H], d_bytes[:].indirect(k2_l[:]))
+        placed = zeroed_bytes(2 * (H + S), "placed", nc.vector)
+        for s in range(4):
+            nc.sync.dma_start(placed[s:P:32, :].bitcast(I32), picked[8 * s : P : 32, :].bitcast(I32))
+        fetch_kinds(PACK - 1)
         n2_l = load_list(n2, "n2_l")
 
-        picked = keep.tile([P, 2 * (H + S)], U8, name="picked", align_bytes=64)
-        dealt = keep.tile([P, 2 * (H + S)], U8, name="dealt", align_bytes=64)
-        nc.vector.tensor_copy(picked[:, 2 * H : 2 * H + S], x_sc[:].indirect(offs_l[:]))
-        nc.vector.tensor_copy(picked[:, 2 * H + S :], x_sc[:].indirect(two_l[:]))
-        nc.vector.tensor_copy(picked[:, :H], d_sc[:].indirect(k1_l[:]))
-        nc.vector.tensor_copy(picked[:, H : 2 * H], d_sc[:].indirect(k2_l[:]))
-        nc.vector.tensor_copy(dealt[:, 2 * H :].bitcast(I32), picked[:, 2 * H :].bitcast(I32))
-        for cols in (slice(0, H), slice(H, 2 * H)):
-            nc.vector.tensor_copy(dealt[:, cols].rearrange("p (t m) -> p m t", t=PACK), picked[:, cols].rearrange("p (m t) -> p m t", t=PACK))
-        placed = zeroed_bytes(2 * (H + S), "placed", nc.gpsimd)
-        for s in range(4):
-            nc.sync.dma_start(placed[s:P:32, :].bitcast(I32), dealt[8 * s : P : 32, :].bitcast(I32))
-
-        def coded_layer(which, k_l, x_l, name, d_at, x_at):
-            picked_words = gather_words(d_w, k_l, name + "_dw_picked", d_at)
-            xw = gather_words(x_w, x_l, name + "_xw", x_at)
-            dw = deal(picked_words[:], I32, name + "_dw", tag=name + "_dw")
-            ds = placed[:, H * which : H * (which + 1)]
-            xs = placed[:, 2 * H + S * which : 2 * H + S * (which + 1)]
+        def coded_layer(layer, k_l, x_l, name, d_tag):
+            d_scale = deal(placed[:, H * layer : H * (layer + 1)], U8, name + "_d_scale")
+            x_scale = placed[:, 2 * H + S * layer : 2 * H + S * (layer + 1)]
+            x_codes = gather_words(x_w, x_l, name + "_x_codes", name + "_x_codes")
+            d_codes = deal(gather_words(d_w, k_l, name + "_d_picked", d_tag)[:], I32, name + "_d_codes")
             banks = []
-            for t in range(PACK):
-                bank = psum.tile([P, S], F32, name=name + "_bank%d" % t, tag="bank%d" % (PACK * which + t))
+            for t in tiles:
+                bank = psum.tile([P, S], F32, name=name + "_bank%d" % t, tag="bank%d" % (PACK * layer + t))
                 cols = slice(P * t, P * (t + 1))
-                nc.tensor.matmul_mx(out=bank[:], lhsT=dw[:, cols].bitcast(FP8X4), lhsT_scale=ds[:, cols],
-                                    rhs=xw[:].bitcast(FP8X4), rhs_scale=xs, start=True, stop=True)
+                nc.tensor.matmul_mx(out=bank[:], lhsT=d_codes[:, cols].bitcast(FP8X4), lhsT_scale=d_scale[:, cols],
+                                    rhs=x_codes[:].bitcast(FP8X4), rhs_scale=x_scale, start=True, stop=True)
                 banks.append(bank)
             return banks
 
-        a_banks = coded_layer(0, k1_l, offs_l, "a", 1024, 3072)
-        b_banks = coded_layer(1, k2_l, two_l, "b", 0, 2048)
+        a_banks = coded_layer(0, k1_l, offs_l, "a", "a_d_picked")
+        b_banks = coded_layer(1, k2_l, two_l, "b", "picked")
 
         w1_in = load_words(w1_words, "w1_in")
         w2_in = load_words(w2_words, "w2_in")
         n4_l = load_list(n4, "n4_l")
-        gm_t = keep.tile([P, PACK], F32, name="gm_t")
-        nc.sync.dma_start(gm_t[:], gm.rearrange("(p t) o -> p (t o)", t=PACK))
-        gn_t = keep.tile([P, PACK], F32, name="gn_t")
-        nc.sync.dma_start(gn_t[:], gn.rearrange("(p t) o -> p (t o)", t=PACK))
+        gm_t = load_gains(gm, "gm_t")
+        gn_t = load_gains(gn, "gn_t")
         n1_l = load_list(n1, "n1_l")
-        w_sc_in = zeroed_bytes(N, "w_sc_in", nc.gpsimd)
-        load_scale_rows(w_sc_in, w1_scales, 0, nc.sync)
-        load_scale_rows(w_sc_in, w2_scales, 4, nc.sync)
+        w_bytes = zeroed_bytes(N, "w_bytes", nc.vector)
+        w1_first, w2_first = 0, 4
+        for src, first in ((w1_scales, w1_first), (w2_scales, w2_first)):
+            for q in range(4):
+                nc.sync.dma_start(w_bytes[32 * q + first : 32 * q + first + 4, :].bitcast(I32),
+                                  src[0, 4 * q : 4 * q + 4, :].bitcast(I32))
         n7_l = load_list(n7, "n7_l")
         n5_l = load_list(n5, "n5_l")
         n6_l = load_list(n6, "n6_l")
 
-        at_n2, diff, size, root, factor = [rows(n) for n in ("at_n2", "diff", "size", "root", "factor")]
-        inner, less_kind, size2 = [rows(n) for n in ("inner", "less_kind", "size2")]
-        at_n4 = late.tile([P, PACK, S], F32, name="at_n4", offset=0)
-        pairs = (slice(0, 2), slice(2, 4))
-        for t in range(PACK):
+        at_n2, diff, diff_size, root, factor = [row_tiles(n) for n in ("at_n2", "diff", "diff_size", "root", "factor")]
+        inner, b_less_tab, inner_size = [row_tiles(n) for n in ("inner", "b_less_tab", "inner_size")]
+        at_n4 = shared.tile([P, PACK, S], F32, name="at_n4", offset=0)
+        for t in tiles:
             nc.scalar.activation(a_rows[t][:, :S], a_banks[t][:], ACT.Copy)
-        for t in range(PACK):
+        for t in tiles:
             if t < N2_ON_SCALAR:
-                fetch(at_n2[:, t, :], a_rows[t], n2_l)
+                scalar_fetch(at_n2[:, t, :], a_rows[t], n2_l[:])
             else:
                 nc.vector.tensor_copy(at_n2[:, t, :], a_rows[t][:].indirect(n2_l[:]))
-        b_rows = [window("b%d" % t) for t in range(PACK)]
-        for t in range(PACK):
+        b_rows = [window("b%d" % t, SCALAR_SPARE) for t in tiles]
+        for t in tiles:
             nc.scalar.activation(b_rows[t][:, :S], b_banks[t][:], ACT.Copy, scale=0.0625)
-        for t in range(PACK):
+        for t in tiles:
             nc.vector.tensor_tensor(diff[:, t, :], at_n2[:, t, :], a_banks[t][:], ALU.subtract)
         for pair in pairs:
-            nc.vector.scalar_tensor_tensor(size[:, pair, :], diff[:, pair, :], -1.0, diff[:, pair, :], ALU.mult, ALU.max)
-        for t in range(PACK):
-            nc.vector.scalar_tensor_tensor(less_kind[:, t, :], b_banks[t][:], 0.0625, kinds[:, t, :], ALU.mult, ALU.subtract)
-        for t in range(PACK):
-            fetch(at_n4[:, t, :], b_rows[t], n4_l)
+            nc.vector.scalar_tensor_tensor(diff_size[:, pair, :], diff[:, pair, :], -1.0, diff[:, pair, :], ALU.mult, ALU.max)
+        for t in tiles:
+            nc.vector.scalar_tensor_tensor(b_less_tab[:, t, :], b_banks[t][:], 0.0625, at_n3[:, t, :], ALU.mult, ALU.subtract)
+        for t in tiles:
+            scalar_fetch(at_n4[:, t, :], b_rows[t], n4_l[:])
         for pair in pairs:
-            nc.vector.tensor_tensor(inner[:, pair, :], less_kind[:, pair, :], at_n4[:, pair, :], ALU.subtract)
+            nc.vector.tensor_tensor(inner[:, pair, :], b_less_tab[:, pair, :], at_n4[:, pair, :], ALU.subtract)
         for pair in pairs:
-            nc.scalar.activation(root[:, pair, :], size[:, pair, :], ACT.Abs_reciprocal_sqrt, bias=8.0)
+            nc.scalar.activation(root[:, pair, :], diff_size[:, pair, :], ACT.Abs_reciprocal_sqrt, bias=8.0)
         for pair in pairs:
-            nc.scalar.activation(size2[:, pair, :], inner[:, pair, :], ACT.Abs)
-        w1_w = deal(w1_in[:], I32, "w1_w", "w1_w")
-        w2_w = deal(w2_in[:], I32, "w2_w", "w2_w")
-        w_sc = keep.tile([P, N], U8, name="w_sc", align_bytes=64)
-        nc.gpsimd.tensor_copy(w_sc[:].rearrange("p (t m) -> p t m", t=PACK), w_sc_in[:].rearrange("p (m t) -> p t m", t=PACK))
-        for t in range(PACK):
+            nc.scalar.activation(inner_size[:, pair, :], inner[:, pair, :], ACT.Abs)
+
+        w1_codes = deal(w1_in[:], I32, "w1_codes")
+        w2_codes = deal(w2_in[:], I32, "w2_codes")
+        w_scale = keep.tile([P, N], U8, name="w_scale", align_bytes=64)
+        nc.gpsimd.tensor_copy(w_scale[:].rearrange("p (t m) -> p t m", t=PACK), w_bytes[:].rearrange("p (m t) -> p t m", t=PACK))
+
+        for t in tiles:
             nc.vector.scalar_tensor_tensor(factor[:, t, :], root[:, t, :], gn_t[:, t : t + 1], root[:, t, :], ALU.mult, ALU.mult)
-        z2_bf = keep.tile([P, PACK * S], BF16, name="z2_bf", align_bytes=64)
+
+        z2_values, z2_codes, z2_scales = mx_tiles("z2")
         gm_wide = gm_t[:].unsqueeze(1).unsqueeze(3).to_broadcast([P, S // 4, PACK, 4])
-        nc.vector.tensor_tensor(woven(z2_bf[:]), by_lines(size2[:]), gm_wide, ALU.mult)
-        z2_codes, z2_plane = quantise(z2_bf, "z2")
-        h_banks = [psum.tile([P, S], F32, name="h_bank%d" % t, tag="bank%d" % (PACK + t)) for t in range(PACK)]
+        nc.vector.tensor_tensor(woven(z2_values[:]), in_fours(inner_size[:]), gm_wide, ALU.mult)
+        quantise(z2_values, z2_codes, z2_scales, whole)
 
-        def product(w_w, first, codes, plane, places, start, stop):
-            for t in range(PACK):
+        h_banks = [psum.tile([P, S], F32, name="h_bank%d" % t, tag="bank%d" % (PACK + t)) for t in tiles]
+
+        def add_product(w_codes, first, codes, scales, places, start, stop):
+            for t in tiles:
                 cols = slice(P * t, P * (t + 1))
-                nc.tensor.matmul_mx(out=h_banks[t][:, places], lhsT=w_w[:, cols].bitcast(FP8X4), lhsT_scale=w_sc[first:P, cols],
-                                    rhs=codes[:, places].bitcast(FP8X4), rhs_scale=plane[:, places], start=start, stop=stop)
+                nc.tensor.matmul_mx(out=h_banks[t][:, places], lhsT=w_codes[:, cols].bitcast(FP8X4), lhsT_scale=w_scale[first:P, cols],
+                                    rhs=codes[:, places].bitcast(FP8X4), rhs_scale=scales[:, places], start=start, stop=stop)
 
-        product(w2_w, 4, z2_codes, z2_plane, slice(0, S), True, False)
-        z_bf = keep.tile([P, PACK * S], BF16, name="z_bf", align_bytes=64)
-        z_codes = keep.tile([P, S], I32, name="z_codes", align_bytes=64)
-        z_plane = keep.tile([P, S], U8, name="z_plane", align_bytes=64)
-        for half in range(2):
-            places = slice(HALF * half, HALF * (half + 1))
-            entries = slice(HALF // 16 * half, HALF // 16 * (half + 1))
-            values = z_bf[:, PACK * HALF * half : PACK * HALF * (half + 1)]
-            at_n1 = late.tile([P, PACK, HALF], F32, name="at_n1_%d" % half, offset=4 * PACK * HALF * half)
+        add_product(w2_codes, w2_first, z2_codes, z2_scales, whole, True, False)
+
+        z_values, z_codes, z_scales = mx_tiles("z")
+        for half, places in enumerate(halves):
+            entries = n1_l[:, places.start // 16 : places.stop // 16]
+            at_n1 = shared.tile([P, PACK, HALF], F32, name="at_n1_%d" % half, offset=4 * PACK * places.start)
             numer = keep.tile([P, PACK, HALF], F32, name="numer%d" % half)
-            for t in range(PACK):
-                nc.scalar.activation(at_n1[:, t, :], a_rows[t][:].indirect(n1_l[:, entries]), ACT.Copy)
+            for t in tiles:
+                scalar_fetch(at_n1[:, t, :], a_rows[t], entries)
                 nc.vector.tensor_tensor(numer[:, t, :], a_banks[t][:, places], at_n1[:, t, :], ALU.subtract)
-            nc.vector.tensor_tensor(woven(values), by_lines(numer[:]), by_lines(factor[:, :, places]), ALU.mult)
-            nc.vector.quantize_mx(out=z_codes[:, places].bitcast(FP8X4), scales=z_plane[:, places], in_=values)
-            product(w1_w, 0, z_codes, z_plane, places, False, half == 1)
+            nc.vector.tensor_tensor(woven(z_values[:, PACK * places.start : PACK * places.stop]), in_fours(numer[:]),
+                                    in_fours(factor[:, :, places]), ALU.mult)
+            quantise(z_values, z_codes, z_scales, places)
+            add_product(w1_codes, w1_first, z_codes, z_scales, places, False, places.stop == S)
 
-        at_n5, at_n7, left, right, result = [rows(n) for n in ("at_n5", "at_n7", "left", "right", "result")]
-        h_rows = [window("h%d" % t) for t in range(PACK)]
-        for t in range(H_ON_VECTOR):
-            nc.vector.tensor_copy(h_rows[t][:, :S], h_banks[t][:])
+        at_n5, at_n6, at_n7, left, right, result = [row_tiles(n) for n in ("at_n5", "at_n6", "at_n7", "left", "right", "result")]
+        h_rows = [window("h%d" % t, VECTOR_SPARE) for t in tiles]
+        for t in tiles:
+            if t % 2 == 0:
+                nc.scalar.activation(h_rows[t][:, :S], h_banks[t][:], ACT.Copy)
+            else:
+                nc.vector.tensor_copy(h_rows[t][:, :S], h_banks[t][:])
+        for t in tiles:
+            nc.vector.tensor_copy(at_n6[:, t, :], h_rows[t][:].indirect(n6_l[:]))
         out_rows = out_0.rearrange("(p t) j -> p t j", t=PACK)
-        y_bf = keep.tile([P, PACK * S], BF16, name="y_bf", align_bytes=64)
-        y_codes = keep.tile([P, S], I32, name="y_codes", align_bytes=64)
-        y_plane = keep.tile([P, S], U8, name="y_plane", align_bytes=64)
-        last = PACK - 1
-        for t in range(PACK):
-            fetch(at_n7[:, t, :], h_rows[t], n7_l)
-            nc.vector.tensor_tensor(right[:, t, :], h_rows[t][:].indirect(n6_l[:]), at_n7[:, t, :], ALU.mult)
-            if t < last:
-                fetch(at_n5[:, t, :], h_rows[t], n5_l)
-                nc.vector.scalar_tensor_tensor(left[:, t, :], h_banks[t][:], 0.75, at_n5[:, t, :], ALU.mult, ALU.mult)
-                nc.vector.scalar_tensor_tensor(result[:, t, :], right[:, t, :], 0.75, left[:, t, :], ALU.mult, ALU.add)
-                nc.sync.dma_start(out_rows[:, t, :], result[:, t, :])
-        fetch(at_n5[:, last, :], h_rows[last], n5_l)
-        nc.vector.scalar_tensor_tensor(left[:, last, :], h_banks[last][:], 0.75, at_n5[:, last, :], ALU.mult, ALU.mult)
-        halves = [slice(HALF * half, HALF * (half + 1)) for half in range(2)]
+        for t in tiles:
+            scalar_fetch(at_n7[:, t, :], h_rows[t], n7_l[:])
+            nc.vector.tensor_tensor(right[:, t, :], at_n6[:, t, :], at_n7[:, t, :], ALU.mult)
+            scalar_fetch(at_n5[:, t, :], h_rows[t], n5_l[:])
+            parts = halves if t == PACK - 1 else (whole,)
+            for places in parts:
+                nc.vector.scalar_tensor_tensor(left[:, t, places], h_banks[t][:, places], 0.75, at_n5[:, t, places], ALU.mult, ALU.mult)
+            for places in parts:
+                nc.vector.scalar_tensor_tensor(result[:, t, places], right[:, t, places], 0.75, left[:, t, places], ALU.mult, ALU.add)
+            nc.sync.dma_start(out_rows[:, t, :], result[:, t, :])
+
+        y_values, y_codes, y_scales = mx_tiles("y")
+        y_pairs = y_values[:].rearrange("p (j u e) -> p u j e", u=2, e=2)
+        result_pairs = result[:].rearrange("p (u e) j -> p u j e", e=2)
+        nc.scalar.copy(y_pairs[:, 0], result_pairs[:, 0])
         for places in halves:
-            nc.vector.scalar_tensor_tensor(result[:, last, places], right[:, last, places], 0.75, left[:, last, places], ALU.mult, ALU.add)
-        nc.sync.dma_start(out_rows[:, last, :], result[:, last, :])
+            nc.vector.tensor_copy(y_pairs[:, 1, places], result_pairs[:, 1, places])
         for places in halves:
-            nc.vector.tensor_copy(woven(y_bf[:, PACK * places.start : PACK * places.stop]), by_lines(result[:, :, places]))
-        for places in halves:
-            nc.vector.quantize_mx(out=y_codes[:, places].bitcast(FP8X4), scales=y_plane[:, places], in_=y_bf[:, PACK * places.start : PACK * places.stop])
+            quantise(y_values, y_codes, y_scales, places)
         nc.sync.dma_start(words_in_hbm(out_1), y_codes[:])
         for q in range(4):
-            (nc.scalar if q < 2 else nc.sync).dma_start(out_2[0, 4 * q : 4 * q + 4, :].bitcast(I32), y_plane[32 * q : 32 * q + 4, :].bitcast(I32))
+            queue = nc.scalar if q < 2 else nc.sync
+            queue.dma_start(out_2[0, 4 * q : 4 * q + 4, :].bitcast(I32), y_scales[32 * q : 32 * q + 4, :].bitcast(I32))

from contextlib import ExitStack

import concourse.mybir as mybir

K, T, S, N, G, H, J = 512, 1024, 256, 512, 2048, 512, 512
FLOPS = 2 * (2 * K * H * S) + 2 * (2 * H * N * S)

F32 = mybir.dt.float32
BF16 = mybir.dt.bfloat16
I32 = mybir.dt.int32
U32 = mybir.dt.uint32
U16 = mybir.dt.uint16
U8 = mybir.dt.uint8
FP8X4 = mybir.dt.float8_e4m3fn_x4
ALU = mybir.AluOpType
ACT = mybir.ActivationFunctionType

P = 128
PACK = 4
HALF = S // 2
SCALAR_SPARE = 8
VECTOR_SPARE = 96
N2_ON_SCALAR = 2


def tile_picked_pqjfrackindddot_none_po_kernel(
    tc, x_words, x_scales, d_words, d_scales, tab, gn, gm, w1_words, w1_scales, w2_words, w2_scales,
    offs, k1, two, k2, n1, n2, n3, n4, n5, n6, n7, out_0, out_1, out_2,
):
    nc = tc.nc
    with ExitStack() as ctx:
        lists = ctx.enter_context(tc.tile_pool(name="lists", bufs=1))
        keep = ctx.enter_context(tc.tile_pool(name="keep", bufs=1))
        shared = ctx.enter_context(tc.tile_pool(name="shared", bufs=1))
        psum = ctx.enter_context(tc.psum_pool(name="psum", bufs=1))

        def load_list(src, name):
            tile = lists.tile(list(src.shape), U16, name=name)
            nc.sync.dma_start(tile[:], src)
            return tile

        def words_in_hbm(src):
            return src[0].rearrange("p n r -> p (n r)").bitcast(I32)

        def load_words(src, name):
            tile = keep.tile([P, src.shape[2]], I32, name=name, align_bytes=64)
            nc.sync.dma_start(tile[:], words_in_hbm(src))
            return tile

        def load_gains(src, name):
            tile = keep.tile([P, PACK], F32, name=name)
            nc.sync.dma_start(tile[:], src.rearrange("(p t) o -> p (t o)", t=PACK))
            return tile

        def zeroed_bytes(width, name, engine):
            tile = keep.tile([P, width], U8, name=name, align_bytes=64)
            engine.memset(tile[:].bitcast(I32), 0)
            return tile

        def deal(src, dtype, name):
            tile = keep.tile([P, H], dtype, name=name, align_bytes=64)
            nc.vector.tensor_copy(tile[:].rearrange("p (t m) -> p m t", t=PACK), src.rearrange("p (m t) -> p m t", t=PACK))
            return tile

        def gather_words(table, offsets, name, tag):
            tile = keep.tile([P, 16 * offsets.shape[1]], I32, name=name, tag=tag, align_bytes=64)
            nc.vector.tensor_copy(tile[:].bitcast(U32), table[:].bitcast(U32).indirect(offsets[:]))
            return tile

        def window(name, spare):
            tile = keep.tile([P, S + spare], F32, name=name)
            nc.vector.memset(tile[:, S:], 0.0)
            return tile

        def row_tiles(name):
            return keep.tile([P, PACK, S], F32, name=name)

        def scalar_fetch(out, src, offsets):
            nc.scalar.activation(out, src[:].indirect(offsets), ACT.Copy)

        def in_fours(ap):
            return ap.rearrange("p t (c i) -> p c t i", i=4)

        def woven(ap):
            return ap.rearrange("p (c i t) -> p c t i", i=4, t=PACK)

        def mx_tiles(name):
            values = keep.tile([P, PACK * S], BF16, name=name + "_bf16", align_bytes=64)
            codes = keep.tile([P, S], I32, name=name + "_codes", align_bytes=64)
            scales = keep.tile([P, S], U8, name=name + "_scales", align_bytes=64)
            return values, codes, scales

        def quantise(values, codes, scales, places):
            nc.vector.quantize_mx(out=codes[:, places].bitcast(FP8X4), scales=scales[:, places],
                                  in_=values[:, PACK * places.start : PACK * places.stop])

        tiles = range(PACK)
        pairs = (slice(0, 2), slice(2, 4))
        halves = (slice(0, HALF), slice(HALF, S))
        whole = slice(0, S)

        x_bytes = zeroed_bytes(T, "x_bytes", nc.gpsimd)
        d_bytes = zeroed_bytes(G, "d_bytes", nc.gpsimd)
        offs_l = load_list(offs, "offs_l")
        nc.sync.dma_start(x_bytes[0:P:8, :].bitcast(I32), x_scales[0].bitcast(I32))
        two_l = load_list(two, "two_l")
        k1_l = load_list(k1, "k1_l")
        k2_l = load_list(k2, "k2_l")
        nc.sync.dma_start(d_bytes[0:P:8, :].bitcast(I32), d_scales[0].bitcast(I32))
        a_rows = [window("a%d" % t, SCALAR_SPARE if t < N2_ON_SCALAR else VECTOR_SPARE) for t in tiles]
        unread = keep.tile([P, 1], F32, name="unread")
        nc.scalar.activation(unread[:], a_rows[0][:, S : S + 1], ACT.Abs_reciprocal_sqrt, bias=8.0)
        x_w = load_words(x_words, "x_w")
        d_w = load_words(d_words, "d_w")
        n3_l = load_list(n3, "n3_l")
        tab_rows = tab.rearrange("(p t) j -> p t j", t=PACK)
        at_n3 = row_tiles("at_n3")

        def fetch_kinds(t):
            tab_t = keep.tile([P, J], F32, name="tab%d" % t)
            nc.sync.dma_start(tab_t[:], tab_rows[:, t, :])
            scalar_fetch(at_n3[:, t, :], tab_t, n3_l[:])

        for t in range(PACK - 1):
            fetch_kinds(t)

        picked = keep.tile([P, 2 * (H + S)], U8, name="picked", tag="picked", align_bytes=64)
        nc.vector.tensor_copy(picked[:, 2 * H : 2 * H + S], x_bytes[:].indirect(offs_l[:]))
        nc.vector.tensor_copy(picked[:, 2 * H + S :], x_bytes[:].indirect(two_l[:]))
        nc.vector.tensor_copy(picked[:, :H], d_bytes[:].indirect(k1_l[:]))
        nc.vector.tensor_copy(picked[:, H : 2 * H], d_bytes[:].indirect(k2_l[:]))
        placed = zeroed_bytes(2 * (H + S), "placed", nc.vector)
        for s in range(4):
            nc.sync.dma_start(placed[s:P:32, :].bitcast(I32), picked[8 * s : P : 32, :].bitcast(I32))
        fetch_kinds(PACK - 1)
        n2_l = load_list(n2, "n2_l")

        def coded_layer(layer, k_l, x_l, name, d_tag):
            d_scale = deal(placed[:, H * layer : H * (layer + 1)], U8, name + "_d_scale")
            x_scale = placed[:, 2 * H + S * layer : 2 * H + S * (layer + 1)]
            x_codes = gather_words(x_w, x_l, name + "_x_codes", name + "_x_codes")
            d_codes = deal(gather_words(d_w, k_l, name + "_d_picked", d_tag)[:], I32, name + "_d_codes")
            banks = []
            for t in tiles:
                bank = psum.tile([P, S], F32, name=name + "_bank%d" % t, tag="bank%d" % (PACK * layer + t))
                cols = slice(P * t, P * (t + 1))
                nc.tensor.matmul_mx(out=bank[:], lhsT=d_codes[:, cols].bitcast(FP8X4), lhsT_scale=d_scale[:, cols],
                                    rhs=x_codes[:].bitcast(FP8X4), rhs_scale=x_scale, start=True, stop=True)
                banks.append(bank)
            return banks

        a_banks = coded_layer(0, k1_l, offs_l, "a", "a_d_picked")
        b_banks = coded_layer(1, k2_l, two_l, "b", "picked")

        w1_in = load_words(w1_words, "w1_in")
        w2_in = load_words(w2_words, "w2_in")
        n4_l = load_list(n4, "n4_l")
        gm_t = load_gains(gm, "gm_t")
        gn_t = load_gains(gn, "gn_t")
        n1_l = load_list(n1, "n1_l")
        w_bytes = zeroed_bytes(N, "w_bytes", nc.vector)
        w1_first, w2_first = 0, 4
        for src, first in ((w1_scales, w1_first), (w2_scales, w2_first)):
            for q in range(4):
                nc.sync.dma_start(w_bytes[32 * q + first : 32 * q + first + 4, :].bitcast(I32),
                                  src[0, 4 * q : 4 * q + 4, :].bitcast(I32))
        n7_l = load_list(n7, "n7_l")
        n5_l = load_list(n5, "n5_l")
        n6_l = load_list(n6, "n6_l")

        at_n2, diff, diff_size, root, factor = [row_tiles(n) for n in ("at_n2", "diff", "diff_size", "root", "factor")]
        inner, b_less_tab, inner_size = [row_tiles(n) for n in ("inner", "b_less_tab", "inner_size")]
        at_n4 = shared.tile([P, PACK, S], F32, name="at_n4", offset=0)
        for t in tiles:
            nc.scalar.activation(a_rows[t][:, :S], a_banks[t][:], ACT.Copy)
        for t in tiles:
            if t < N2_ON_SCALAR:
                scalar_fetch(at_n2[:, t, :], a_rows[t], n2_l[:])
            else:
                nc.vector.tensor_copy(at_n2[:, t, :], a_rows[t][:].indirect(n2_l[:]))
        b_rows = [window("b%d" % t, SCALAR_SPARE) for t in tiles]
        for t in tiles:
            nc.scalar.activation(b_rows[t][:, :S], b_banks[t][:], ACT.Copy, scale=0.0625)
        for t in tiles:
            nc.vector.tensor_tensor(diff[:, t, :], at_n2[:, t, :], a_banks[t][:], ALU.subtract)
        for pair in pairs:
            nc.vector.scalar_tensor_tensor(diff_size[:, pair, :], diff[:, pair, :], -1.0, diff[:, pair, :], ALU.mult, ALU.max)
        for t in tiles:
            nc.vector.scalar_tensor_tensor(b_less_tab[:, t, :], b_banks[t][:], 0.0625, at_n3[:, t, :], ALU.mult, ALU.subtract)
        for t in tiles:
            scalar_fetch(at_n4[:, t, :], b_rows[t], n4_l[:])
        for pair in pairs:
            nc.vector.tensor_tensor(inner[:, pair, :], b_less_tab[:, pair, :], at_n4[:, pair, :], ALU.subtract)
        for pair in pairs:
            nc.scalar.activation(root[:, pair, :], diff_size[:, pair, :], ACT.Abs_reciprocal_sqrt, bias=8.0)
        for pair in pairs:
            nc.scalar.activation(inner_size[:, pair, :], inner[:, pair, :], ACT.Abs)

        w1_codes = deal(w1_in[:], I32, "w1_codes")
        w2_codes = deal(w2_in[:], I32, "w2_codes")
        w_scale = keep.tile([P, N], U8, name="w_scale", align_bytes=64)
        nc.gpsimd.tensor_copy(w_scale[:].rearrange("p (t m) -> p t m", t=PACK), w_bytes[:].rearrange("p (m t) -> p t m", t=PACK))

        for t in tiles:
            nc.vector.scalar_tensor_tensor(factor[:, t, :], root[:, t, :], gn_t[:, t : t + 1], root[:, t, :], ALU.mult, ALU.mult)

        z2_values, z2_codes, z2_scales = mx_tiles("z2")
        gm_wide = gm_t[:].unsqueeze(1).unsqueeze(3).to_broadcast([P, S // 4, PACK, 4])
        nc.vector.tensor_tensor(woven(z2_values[:]), in_fours(inner_size[:]), gm_wide, ALU.mult)
        quantise(z2_values, z2_codes, z2_scales, whole)

        h_banks = [psum.tile([P, S], F32, name="h_bank%d" % t, tag="bank%d" % (PACK + t)) for t in tiles]

        def add_product(w_codes, first, codes, scales, places, start, stop):
            for t in tiles:
                cols = slice(P * t, P * (t + 1))
                nc.tensor.matmul_mx(out=h_banks[t][:, places], lhsT=w_codes[:, cols].bitcast(FP8X4), lhsT_scale=w_scale[first:P, cols],
                                    rhs=codes[:, places].bitcast(FP8X4), rhs_scale=scales[:, places], start=start, stop=stop)

        add_product(w2_codes, w2_first, z2_codes, z2_scales, whole, True, False)

        z_values, z_codes, z_scales = mx_tiles("z")
        for half, places in enumerate(halves):
            entries = n1_l[:, places.start // 16 : places.stop // 16]
            at_n1 = shared.tile([P, PACK, HALF], F32, name="at_n1_%d" % half, offset=4 * PACK * places.start)
            numer = keep.tile([P, PACK, HALF], F32, name="numer%d" % half)
            for t in tiles:
                scalar_fetch(at_n1[:, t, :], a_rows[t], entries)
                nc.vector.tensor_tensor(numer[:, t, :], a_banks[t][:, places], at_n1[:, t, :], ALU.subtract)
            nc.vector.tensor_tensor(woven(z_values[:, PACK * places.start : PACK * places.stop]), in_fours(numer[:]),
                                    in_fours(factor[:, :, places]), ALU.mult)
            quantise(z_values, z_codes, z_scales, places)
            add_product(w1_codes, w1_first, z_codes, z_scales, places, False, places.stop == S)

        at_n5, at_n6, at_n7, left, right, result = [row_tiles(n) for n in ("at_n5", "at_n6", "at_n7", "left", "right", "result")]
        h_rows = [window("h%d" % t, VECTOR_SPARE) for t in tiles]
        for t in tiles:
            if t % 2 == 0:
                nc.scalar.activation(h_rows[t][:, :S], h_banks[t][:], ACT.Copy)
            else:
                nc.vector.tensor_copy(h_rows[t][:, :S], h_banks[t][:])
        for t in tiles:
            nc.vector.tensor_copy(at_n6[:, t, :], h_rows[t][:].indirect(n6_l[:]))
        out_rows = out_0.rearrange("(p t) j -> p t j", t=PACK)
        for t in tiles:
            scalar_fetch(at_n7[:, t, :], h_rows[t], n7_l[:])
            nc.vector.tensor_tensor(right[:, t, :], at_n6[:, t, :], at_n7[:, t, :], ALU.mult)
            scalar_fetch(at_n5[:, t, :], h_rows[t], n5_l[:])
            parts = halves if t == PACK - 1 else (whole,)
            for places in parts:
                nc.vector.scalar_tensor_tensor(left[:, t, places], h_banks[t][:, places], 0.75, at_n5[:, t, places], ALU.mult, ALU.mult)
            for places in parts:
                nc.vector.scalar_tensor_tensor(result[:, t, places], right[:, t, places], 0.75, left[:, t, places], ALU.mult, ALU.add)
            nc.sync.dma_start(out_rows[:, t, :], result[:, t, :])

        y_values, y_codes, y_scales = mx_tiles("y")
        y_pairs = y_values[:].rearrange("p (j u e) -> p u j e", u=2, e=2)
        result_pairs = result[:].rearrange("p (u e) j -> p u j e", e=2)
        nc.scalar.copy(y_pairs[:, 0], result_pairs[:, 0])
        for places in halves:
            nc.vector.tensor_copy(y_pairs[:, 1, places], result_pairs[:, 1, places])
        for places in halves:
            quantise(y_values, y_codes, y_scales, places)
        nc.sync.dma_start(words_in_hbm(out_1), y_codes[:])
        for q in range(4):
            queue = nc.scalar if q < 2 else nc.sync
            queue.dma_start(out_2[0, 4 * q : 4 * q + 4, :].bitcast(I32), y_scales[32 * q : 32 * q + 4, :].bitcast(I32))
